import numpy as np
import ml_dtypes


def mxq(x, axis, fmt="e4m3"):
    dtype, down = {"e4m3": (ml_dtypes.float8_e4m3fn, 7), "e5m2": (ml_dtypes.float8_e5m2, 14)}[fmt]
    v = np.moveaxis(np.asarray(x, np.float32).astype(ml_dtypes.bfloat16).astype(np.float64), axis, -1)
    blocks = v.reshape(v.shape[:-1] + (-1, 32))
    amax = np.abs(blocks).max(-1, keepdims=True)
    byte = np.maximum(np.where(amax > 0, np.frexp(amax)[1] - 1 + 127, 0) - down, 1)
    scale = np.exp2(byte - 127.0)
    codes = (blocks / scale).astype(np.float32).astype(dtype).astype(np.float64)
    return np.moveaxis((codes * scale).reshape(v.shape), -1, axis)


WIDE = False


def mx_kscale(k):
    if not WIDE:
        return np.ones(k)
    levels = np.array([10, -10, 5, -5, 0])
    if k % 512:
        return np.exp2(np.random.permutation(np.resize(levels, k // 32))).repeat(32)
    a = np.empty((k // 512, 16))
    for p in range(k // 512):
        a[p, :8] = np.random.permutation(np.resize(levels, 8))
        for g in range(8):
            far = levels[np.abs(levels - a[p, g]) >= 10]
            a[p, g + 8] = far[np.random.randint(len(far))]
    return np.exp2(a.ravel()).repeat(32)


def f64(x):
    return np.asarray(x).astype(np.float64)


def striped(idx):
    return np.tile(idx.reshape(-1, 16).T, (8, 1)).astype(np.uint16)


def unstriped(offs):
    return offs[:16].T.reshape(-1).astype(np.int64)


E2M1 = np.array([0.0, 0.5, 1.0, 1.5, 2.0, 3.0, 4.0, 6.0, -0.0, -0.5, -1.0, -1.5, -2.0, -3.0, -4.0, -6.0])


def pack_weight(w, fmt):
    k, n = w.shape
    w = f64(np.asarray(w, np.float32).astype(ml_dtypes.bfloat16)).reshape(k // 32, 32, n)
    amax = np.abs(w).max(1)
    if fmt == "e4m3":
        byte = np.frexp(amax)[1] - 1 + 127 - 7
    else:
        mant, ex = np.frexp(amax / 6.0)
        byte = np.where(mant > 0.5, ex, ex - 1) + 127
    byte = np.clip(np.where(amax > 0, byte, 1), 1, 254)
    scaled = (w * np.exp2(127.0 - byte)[:, None, :]).reshape(k, n).astype(np.float32)
    by_word = np.ascontiguousarray(scaled.reshape(k // 512, 128, 4, n).transpose(0, 1, 3, 2))
    if fmt == "e4m3":
        words = by_word.astype(ml_dtypes.float8_e4m3fn).view(np.uint8)
    else:
        c = by_word.astype(ml_dtypes.float4_e2m1fn).view(np.uint8) & 0xF
        words = (c[..., 0::2] | (c[..., 1::2] << 4)).reshape(k // 512, 128, 2 * n)
    return np.ascontiguousarray(words), np.ascontiguousarray(byte.astype(np.uint8).reshape(k // 512, 16, n))


def unpack_weight(words, scales, fmt):
    g, _, n = scales.shape
    words = np.ascontiguousarray(words).reshape(g, 128, n, -1)
    if fmt == "e4m3":
        vals = words.view(ml_dtypes.float8_e4m3fn).astype(np.float64)
    else:
        nib = np.empty((g, 128, n, 4), np.uint8)
        nib[..., 0::2] = words & 0xF
        nib[..., 1::2] = words >> 4
        vals = E2M1[nib]
    vals = vals * np.repeat(np.exp2(scales.astype(np.float64) - 127.0), 8, axis=1)[..., None]
    return vals.transpose(0, 1, 3, 2).reshape(g * 512, n)


def gelu(v):
    return 0.5 * v * (1.0 + np.tanh(np.sqrt(2.0 / np.pi) * (v + 0.044715 * v**3)))


K, H, T, S, T2, P, T3, S2 = 1024, 1024, 2048, 512, 1024, 512, 2048, 1024

def setup_inputs():
    n = np.random.standard_normal
    u = mx_kscale(H)[:, None]
    d = {}
    d["tab_words"], d["tab_scales"] = pack_weight(0.6 * n((K, T)) * u, "e4m3")
    d["offs"] = striped(np.random.permutation(T)[:S])
    d["tab2_words"], d["tab2_scales"] = pack_weight(1.1 * n((H, T3)) / np.sqrt(H) / u, "e4m3")
    d["offs2"] = striped(np.random.permutation(T3)[:S2])
    d["w1_words"], d["w1_scales"] = pack_weight(2.5 * n((K, H)) / np.sqrt(K) / u, "e2m1")
    d["w2"] = (0.95 * n((K, H)) / np.sqrt(K) / u).astype(np.float32)
    d["w3"] = (0.85 * n((K, H)) / np.sqrt(K) / u * u.T).astype(np.float32)
    d["gain"] = (1.4 * np.exp(0.3 * n(H)) * u[:, 0]).astype(np.float32)
    d["page0"] = (0.9 * n((H, T2)) * u).astype(np.float32)
    d["wgs"] = np.exp(0.3 * n((128, S))).astype(np.float32)
    d["offs3"] = striped(np.random.permutation(T2)[:S])
    d["offs4"] = striped(np.random.permutation(T2)[:P])
    d["base"] = ((0.6 * n(H) - 0.2) * u[:, 0]).astype(np.float32)
    return d

def reference(tab_words, tab_scales, offs, tab2_words, tab2_scales, offs2, w1_words, w1_scales, w2, w3, gain, page0, wgs, offs3, offs4, base):
    v = unpack_weight(tab_words, tab_scales, "e4m3")[:, unstriped(offs)]
    v2 = unpack_weight(tab2_words, tab2_scales, "e4m3")[:, unstriped(offs2)]
    w1 = unpack_weight(w1_words, w1_scales, "e2m1")
    a = w1.T @ v
    b = mxq(f64(w2), 0, "e4m3").T @ v
    d = mxq(f64(w3), 0, "e4m3").T @ v
    h = f64(gain)[:, None] * np.tanh(a) * np.cos(b) + d
    page = f64(page0).copy()
    page[:, unstriped(offs3)] = np.tile(f64(wgs), (H // 128, 1)) * h
    x = np.maximum(page[:, unstriped(offs4)], f64(base)[:, None])
    e = v2.T @ mxq(x, 0, "e4m3") + v2.T @ v
    return np.tanh(e)

@@ -1,0 +1,302 @@
+import math
+from contextlib import ExitStack
+
+import concourse.mybir as mybir
+
+F32 = mybir.dt.float32
+BF16 = mybir.dt.bfloat16
+I32 = mybir.dt.int32
+U32 = mybir.dt.uint32
+U16 = mybir.dt.uint16
+U8 = mybir.dt.uint8
+FP8X4 = mybir.dt.float8_e4m3fn_x4
+FP4X4 = mybir.dt.float4_e2m1fn_x4
+ACT = mybir.ActivationFunctionType
+ALU = mybir.AluOpType
+
+P = 128
+PACK = 4
+PASS = P * PACK
+K = 1024
+T = 2048
+S = 512
+S2 = 1024
+T2 = 1024
+NPASS = K // PASS
+SLICE = 256
+
+FLOPS = 5368709120
+
+
+def tile_list_shelf_offer_scores_kernel(
+    tc, tab_words, tab_scales, offs, tab2_words, tab2_scales, offs2, w1_words, w1_scales,
+    w2, w3, gain, page0, wgs, offs3, offs4, base, out,
+):
+    nc = tc.nc
+    with ExitStack() as ctx:
+        keep = ctx.enter_context(tc.tile_pool(name="keep", bufs=1))
+        ring = ctx.enter_context(tc.tile_pool(name="ring", bufs=2))
+        psum = ctx.enter_context(tc.psum_pool(name="psum", bufs=1))
+
+        def load_list(name, src):
+            t = keep.tile(list(src.shape), U16, name=name)
+            nc.sync.dma_start(t[:], src)
+            return t
+
+        def load_words(name, src):
+            t = keep.tile([P, T], I32, name=name)
+            nc.sync.dma_start(t[:], src.rearrange("p t i -> p (t i)").bitcast(I32))
+            return t
+
+        def zeroed_planes(name, shape):
+            t = keep.tile(shape, U8, name=name, align_bytes=64)
+            nc.vector.memset(t[:].bitcast(I32), 0)
+            return t
+
+        def load_planes(t, src):
+            for r in range(4):
+                nc.sync.dma_start(
+                    t[r:P:32].bitcast(I32), src[:, r:16:4, :].rearrange("a q c -> q a c").bitcast(I32)
+                )
+
+        def load_weight(w, a, b):
+            raw = ring.tile([P, PACK, PASS], F32, name="w_raw", bufs=4)
+            nc.sync.dma_start(
+                raw[:], w[a * PASS:(a + 1) * PASS, b * PASS:(b + 1) * PASS].rearrange("(p j) c -> p j c", j=PACK)
+            )
+            return raw
+
+        def load_page(b, t):
+            page = keep.tile([P, T2], F32, name=f"page{b}{t}")
+            nc.sync.dma_start(page[:], page0[b * PASS + t:(b + 1) * PASS:PACK, :])
+            return page
+
+
+        tab_planes = zeroed_planes("tab_planes", [P, NPASS, T])
+        w1_planes_raw = zeroed_planes("w1_planes_raw", [P, NPASS, K])
+        tab2_planes = zeroed_planes("tab2_planes", [P, T])
+
+        gain_sb = keep.tile([P, NPASS, PACK], F32, name="gain_sb")
+        base_sb = keep.tile([P, NPASS, PACK], F32, name="base_sb")
+
+        list1 = load_list("list1", offs)
+        tab_w = [load_words("tab_w0", tab_words[0])]
+        load_planes(tab_planes, tab_scales)
+        raw2 = {(0, 0): load_weight(w2, 0, 0)}
+        tab_w.append(load_words("tab_w1", tab_words[1]))
+        w1_raw = keep.tile([P, NPASS, 2 * K], U8, name="w1_raw", align_bytes=64)
+        nc.sync.dma_start(w1_raw[:].bitcast(I32), w1_words.rearrange("a p c -> p a c").bitcast(I32))
+        load_planes(w1_planes_raw, w1_scales)
+        raw2[1, 0] = load_weight(w2, 1, 0)
+        raw3 = {(0, 0): load_weight(w3, 0, 0)}
+        nc.sync.dma_start(gain_sb[:], gain.rearrange("(b p t) -> p b t", p=P, t=PACK))
+        raw3[1, 0] = load_weight(w3, 1, 0)
+        list3 = load_list("list3", offs3)
+        wgs_sb = keep.tile([P, PACK, S], F32, name="wgs_sb")
+        for q in (0, 2, 1, 3):
+            nc.sync.dma_start(wgs_sb[32 * q:32 * q + 32], wgs.rearrange("(p t) j -> p t j", t=PACK))
+        pages = {(0, 0): load_page(0, 0)}
+        list4 = load_list("list4", offs4)
+        nc.sync.dma_start(base_sb[:], base.rearrange("(b p t) -> p b t", p=P, t=PACK))
+
+        v_words, v_planes = [], []
+        for a in range(NPASS):
+            words = keep.tile([P, S], U32, name=f"v_words{a}", align_bytes=64)
+            plane = keep.tile([P, S], U8, name=f"v_plane{a}", align_bytes=64)
+            nc.vector.tensor_copy(words[:], tab_w[a][:].bitcast(U32).indirect(list1[:]))
+            nc.vector.tensor_copy(plane[:], tab_planes[:, a, :].indirect(list1[:]))
+            v_words.append(words)
+            v_planes.append(plane)
+
+        w1_dealt = keep.tile([P, NPASS * 2 * K], U8, name="w1_dealt", align_bytes=64)
+        w1_planes = keep.tile([P, NPASS * K], U8, name="w1_planes", align_bytes=64)
+        nc.vector.tensor_copy(
+            w1_dealt[:].bitcast(U16).rearrange("p (g t m) -> p g t m", t=PACK, m=P),
+            w1_raw[:].rearrange("p a c -> p (a c)").bitcast(U16).rearrange("p (g m t) -> p g t m", t=PACK, m=P),
+        )
+        nc.vector.tensor_copy(
+            w1_planes[:].rearrange("p (g t m) -> p g t m", t=PACK, m=P),
+            w1_planes_raw[:].rearrange("p a (b m t) -> p (a b) t m", t=PACK, m=P),
+        )
+
+        def quantise(grouped, name, width):
+            words = keep.tile([P, width], U32, name=f"{name}_words", align_bytes=64)
+            plane = keep.tile([P, width], U8, name=f"{name}_plane", align_bytes=64)
+            nc.vector.quantize_mx(out=words[:].bitcast(FP8X4), scales=plane[:], in_=grouped[:])
+            return words, plane
+
+        def quantise_weight(raw, name, cast):
+            grouped = ring.tile([P, PACK * PASS], BF16, name="w_grouped", align_bytes=64, bufs=3)
+            cast(
+                grouped[:].rearrange("p (t m j) -> p m t j", t=PACK, j=PACK),
+                raw[:].rearrange("p j (m t) -> p m t j", t=PACK),
+            )
+            return quantise(grouped, name, PASS)
+
+        def product(bank, stationary):
+            acc = psum.tile([P, S], F32, name=f"bank{bank}")
+            for a in range(NPASS):
+                words, plane = stationary(a)
+                nc.tensor.matmul_mx(
+                    out=acc[:], lhsT=words, lhsT_scale=plane,
+                    rhs=v_words[a][:].bitcast(FP8X4), rhs_scale=v_planes[a][:],
+                    start=(a == 0), stop=(a == NPASS - 1),
+                )
+            return acc
+
+        def w1_tile(b, t):
+            def at(a):
+                c = ((a * NPASS + b) * PACK + t) * P
+                return w1_dealt[:, 2 * c:2 * (c + P)].bitcast(FP4X4), w1_planes[:, c:c + P]
+            return at
+
+        def wq_tile(q, b, t):
+            def at(a):
+                words, plane = q[a, b]
+                return words[:, t * P:(t + 1) * P].bitcast(FP8X4), plane[:, t * P:(t + 1) * P]
+            return at
+
+        q2, q3, th, turns, whole, cosb, tanh_cos, acc_d, h, picked = ({} for n in range(10))
+        TILES = NPASS * PACK
+
+        def drain_ab(i):
+            b, t = divmod(i, PACK)
+            acc_b = product(2 + i % 2, wq_tile(q2, b, t))
+            acc_a = product(4 + i % 2, w1_tile(b, t))
+            turns[i] = ring.tile([P, S], F32, name="turns", bufs=4)
+            whole[i] = ring.tile([P, S], U32, name="whole", bufs=4)
+            th[i] = ring.tile([P, S], F32, name="th", bufs=4)
+            nc.scalar.activation(turns[i][:], acc_b[:], ACT.Abs, scale=1.0 / (2.0 * math.pi))
+            nc.scalar.activation(whole[i][:], turns[i][:], ACT.Copy, bias=0.25)
+            nc.scalar.activation(th[i][:], acc_a[:], ACT.Tanh)
+
+        def cosine(i):
+            cosb[i] = keep.tile([P, S], F32, name=f"cosb{min(i, PACK - 1)}")
+            nc.vector.scalar_tensor_tensor(cosb[i][:], turns[i][:], 0.25, whole[i][:].bitcast(I32), ALU.add, ALU.subtract)
+            nc.scalar.activation(cosb[i][:], cosb[i][:], ACT.Sin, scale=2.0 * math.pi)
+
+        def tanh_times_cos(i):
+            tanh_cos[i] = keep.tile([P, S], F32, name=f"tanh_cos{min(i, PACK - 1)}")
+            nc.vector.tensor_tensor(tanh_cos[i][:], th[i][:], cosb[i][:], ALU.mult)
+
+        def make_h(i):
+            b, t = divmod(i, PACK)
+            acc = product(6 + i % 2, wq_tile(q3, b, t))
+            h[i] = keep.tile([P, S], F32, name="h", align_bytes=64)
+            nc.vector.scalar_tensor_tensor(h[i][:], tanh_cos[i][:], gain_sb[:, b, t:t + 1], acc[:], ALU.mult, ALU.add)
+
+        def scatter(i):
+            b, t = divmod(i, PACK)
+            nc.vector.tensor_tensor(pages[b, t][:].indirect(list3[:]), h[i][:], wgs_sb[:, t, :], ALU.mult)
+
+        def pick(i):
+            picked[i] = keep.tile([P, S], F32, name="picked", align_bytes=64)
+            nc.vector.tensor_copy(picked[i][:], pages[divmod(i, PACK)][:].indirect(list4[:]))
+
+        def floor_at_base(i):
+            b, t = divmod(i, PACK)
+            nc.vector.tensor_scalar(x_planes[b][:, t, :], picked[i][:], base_sb[:, b, t:t + 1], None, ALU.max)
+
+        def interleave_x(b, shares):
+            grouped = keep.tile([P, S * PACK], BF16, name="x_grouped", align_bytes=64)
+            for copy, j0, j1 in shares:
+                copy(
+                    grouped[:, j0 * PACK:j1 * PACK].rearrange("p (c i t) -> p c t i", i=4, t=PACK),
+                    x_planes[b][:, :, j0:j1].rearrange("p t (c i) -> p c t i", i=4),
+                )
+            return grouped
+
+        x_planes = [ring.tile([P, PACK, S], BF16, name="x_planes") for b in range(NPASS)]
+        xq = []
+
+        q2[0, 0] = quantise_weight(raw2[0, 0], "w2_00", nc.scalar.copy)
+        q2[1, 0] = quantise_weight(raw2[1, 0], "w2_10", nc.vector.tensor_copy)
+        for i in range(PACK):
+            drain_ab(i)
+            cosine(i)
+            tanh_times_cos(i)
+            if i == 0:
+                for a in range(NPASS):
+                    q3[a, 0] = quantise_weight(raw3[a, 0], f"w3_{a}0", nc.vector.tensor_copy)
+        for a in range(NPASS):
+            raw2[a, 1] = load_weight(w2, a, 1)
+        pages[0, 1] = load_page(0, 1)
+        for a in range(NPASS):
+            raw3[a, 1] = load_weight(w3, a, 1)
+        list2 = load_list("list2", offs2)
+        tab2_w = [load_words("tab_w0", tab2_words[0])]
+        pages[0, 2] = load_page(0, 2)
+        for q in range(4):
+            nc.sync.dma_start(
+                tab2_planes[32 * q:32 * q + 8, :].bitcast(I32), tab2_scales[:, 4 * q:4 * q + 4, :].bitcast(I32)
+            )
+        pages[0, 3] = load_page(0, 3)
+        for t in range(PACK):
+            pages[1, t] = load_page(1, t)
+        tab2_w.append(load_words("tab_w1", tab2_words[1]))
+
+        for a in range(NPASS):
+            q2[a, 1] = quantise_weight(raw2[a, 1], f"w2_{a}1", nc.scalar.copy)
+        for i in range(PACK, TILES):
+            drain_ab(i)
+            if i == PACK:
+                cosine(i)
+                for a in range(NPASS):
+                    q3[a, 1] = quantise_weight(raw3[a, 1], f"w3_{a}1", nc.scalar.copy)
+
+        half = S2 // 2
+        v2_plane = keep.tile([P, S2], U8, name="v2_plane", align_bytes=64)
+
+        def gather_v2(name, a, m0, count):
+            dst = keep.tile([P, count], U32, name=name, align_bytes=64)
+            for c in range(0, count, SLICE if a else half):
+                n = SLICE if a else half
+                part = list2[:, (m0 + c) // 16:(m0 + c + n) // 16]
+                nc.vector.tensor_copy(dst[:, c:c + n], tab2_w[a][:].bitcast(U32).indirect(part))
+            for c in range(0, count, P):
+                v2_words[a, (m0 + c) // P] = dst[:, c:c + P]
+
+        v2_words = {}
+        make_h(0)
+        for i in range(TILES):
+            scatter(i)
+            if i + 1 < TILES:
+                make_h(i + 1)
+            else:
+                gather_v2("h", 0, half, half)
+            pick(i)
+            if PACK <= i + 2 < TILES:
+                tanh_times_cos(i + 2)
+            floor_at_base(i)
+            if PACK < i + 3 < TILES:
+                cosine(i + 3)
+            if i == PACK - 1:
+                xq.append(quantise(interleave_x(0, [(nc.scalar.copy, 0, S)]), "x0", S))
+            if i == PACK:
+                nc.vector.tensor_copy(v2_plane[:], tab2_planes[:].indirect(list2[:]))
+                gather_v2("v2_early", 0, 0, half)
+
+        grouped = interleave_x(1, [(nc.scalar.copy, 0, S // 2), (nc.vector.tensor_copy, S // 2, S)])
+        gather_v2("picked", 1, 0, SLICE)
+        xq.append(quantise(grouped, "x1", S))
+        gather_v2("x_grouped", 1, SLICE, S2 - SLICE)
+
+        acc_e = [psum.tile([P, S], F32, name=f"bank{m}") for m in range(S2 // P)]
+
+        def score_pass(m, a, moving, start=False, stop=False):
+            nc.tensor.matmul_mx(
+                out=acc_e[m][:], lhsT=v2_words[a, m].bitcast(FP8X4), lhsT_scale=v2_plane[4 * a:P, m * P:(m + 1) * P],
+                rhs=moving[0][:].bitcast(FP8X4), rhs_scale=moving[1][:], start=start, stop=stop,
+            )
+
+        vq = list(zip(v_words, v_planes))
+        for m in range(8):
+            score_pass(m, 0, vq[0], start=True)
+            score_pass(m, 0, xq[0])
+        for m in range(8):
+            score_pass(m, 1, vq[1])
+            score_pass(m, 1, xq[1], stop=True)
+            if m % 2 == 0:
+                res = ring.tile([P, 2, S], F32, name="w_raw", bufs=4)
+            nc.scalar.activation(res[:, m % 2, :], acc_e[m][:], ACT.Tanh)
+            nc.sync.dma_start(out[m * P:(m + 1) * P, :], res[:, m % 2, :])

@@ -71,6 +71,9 @@ def tile_list_shelf_offer_scores_kernel(
             nc.sync.dma_start(page[:], page0[b * PASS + t:(b + 1) * PASS:PACK, :])
             return page
 
+        warm = keep.tile([P, 2], F32, name="warm")
+        nc.vector.memset(warm[:, 0:1], 0.0)
+        nc.scalar.activation(warm[:, 1:2], warm[:, 0:1], ACT.Silu)
 
         tab_planes = zeroed_planes("tab_planes", [P, NPASS, T])
         w1_planes_raw = zeroed_planes("w1_planes_raw", [P, NPASS, K])

@@ -2,6 +2,7 @@ import math
 from contextlib import ExitStack
 
 import concourse.mybir as mybir
+from concourse.masks import make_identity
 
 F32 = mybir.dt.float32
 BF16 = mybir.dt.bfloat16
@@ -59,46 +60,65 @@ def tile_list_shelf_offer_scores_kernel(
                     t[r:P:32].bitcast(I32), src[:, r:16:4, :].rearrange("a q c -> q a c").bitcast(I32)
                 )
 
+        staged = []
+
         def load_weight(w, a, b):
-            raw = ring.tile([P, PACK, PASS], F32, name="w_raw", bufs=4)
+            raw = keep.tile([P, PACK, PASS], F32, name=f"stage{len(staged) % 4}")
+            staged.append(raw)
             nc.sync.dma_start(
                 raw[:], w[a * PASS:(a + 1) * PASS, b * PASS:(b + 1) * PASS].rearrange("(p j) c -> p j c", j=PACK)
             )
             return raw
 
         def load_page(b, t):
-            page = keep.tile([P, T2], F32, name=f"page{b}{t}")
+            page = keep.tile([P, T2], F32, name=f"page{b}{t}", align_bytes=64)
             nc.sync.dma_start(page[:], page0[b * PASS + t:(b + 1) * PASS:PACK, :])
             return page
 
+        tab_planes = keep.tile([P, NPASS, T], U8, name="tab_planes", align_bytes=64)
+        nc.vector.memset(tab_planes[:, 0, :].bitcast(I32), 0)
+        nc.gpsimd.memset(tab_planes[:, 1, :].bitcast(I32), 0)
         warm = keep.tile([P, 2], F32, name="warm")
-        nc.vector.memset(warm[:, 0:1], 0.0)
+        nc.gpsimd.memset(warm[:, 0:1], 0.0)
         nc.scalar.activation(warm[:, 1:2], warm[:, 0:1], ACT.Silu)
 
-        tab_planes = zeroed_planes("tab_planes", [P, NPASS, T])
-        w1_planes_raw = zeroed_planes("w1_planes_raw", [P, NPASS, K])
         tab2_planes = zeroed_planes("tab2_planes", [P, T])
+        w1_planes_raw = zeroed_planes("w1_planes_raw", [P, NPASS, K])
+
+        ident = keep.tile([P, P], F32, name="ident")
+        make_identity(nc, ident[:])
 
         gain_sb = keep.tile([P, NPASS, PACK], F32, name="gain_sb")
         base_sb = keep.tile([P, NPASS, PACK], F32, name="base_sb")
 
-        list1 = load_list("list1", offs)
+        raw2 = {}
         tab_w = [load_words("tab_w0", tab_words[0])]
+        list1 = load_list("list1", offs)
         load_planes(tab_planes, tab_scales)
-        raw2 = {(0, 0): load_weight(w2, 0, 0)}
+        raw2[0, 0] = load_weight(w2, 0, 0)
+        list2 = load_list("list2", offs2)
+        for q in range(4):
+            nc.sync.dma_start(
+                tab2_planes[32 * q:32 * q + 8, :].bitcast(I32), tab2_scales[:, 4 * q:4 * q + 4, :].bitcast(I32)
+            )
+        raw2[1, 0] = load_weight(w2, 1, 0)
         tab_w.append(load_words("tab_w1", tab_words[1]))
         w1_raw = keep.tile([P, NPASS, 2 * K], U8, name="w1_raw", align_bytes=64)
         nc.sync.dma_start(w1_raw[:].bitcast(I32), w1_words.rearrange("a p c -> p a c").bitcast(I32))
         load_planes(w1_planes_raw, w1_scales)
-        raw2[1, 0] = load_weight(w2, 1, 0)
         raw3 = {(0, 0): load_weight(w3, 0, 0)}
         nc.sync.dma_start(gain_sb[:], gain.rearrange("(b p t) -> p b t", p=P, t=PACK))
         raw3[1, 0] = load_weight(w3, 1, 0)
         list3 = load_list("list3", offs3)
-        wgs_sb = keep.tile([P, PACK, S], F32, name="wgs_sb")
+        wgs_rows = wgs.rearrange("(p t) j -> p t j", t=PACK)
+        wgs_first = keep.tile([P, 1, S], F32, name="wgs_first")
+        wgs_rest = keep.tile([P, PACK - 1, S], F32, name="wgs_rest")
+        wgs_sb = [wgs_first[:, 0, :]] + [wgs_rest[:, t, :] for t in range(PACK - 1)]
         for q in (0, 2, 1, 3):
-            nc.sync.dma_start(wgs_sb[32 * q:32 * q + 32], wgs.rearrange("(p t) j -> p t j", t=PACK))
+            nc.sync.dma_start(wgs_first[32 * q:32 * q + 32], wgs_rows[:, 0:1, :])
         pages = {(0, 0): load_page(0, 0)}
+        for q in (0, 2, 1, 3):
+            nc.sync.dma_start(wgs_rest[32 * q:32 * q + 32], wgs_rows[:, 1:PACK, :])
         list4 = load_list("list4", offs4)
         nc.sync.dma_start(base_sb[:], base.rearrange("(b p t) -> p b t", p=P, t=PACK))
 
@@ -111,29 +131,23 @@ def tile_list_shelf_offer_scores_kernel(
             v_words.append(words)
             v_planes.append(plane)
 
-        w1_dealt = keep.tile([P, NPASS * 2 * K], U8, name="w1_dealt", align_bytes=64)
-        w1_planes = keep.tile([P, NPASS * K], U8, name="w1_planes", align_bytes=64)
-        nc.vector.tensor_copy(
-            w1_dealt[:].bitcast(U16).rearrange("p (g t m) -> p g t m", t=PACK, m=P),
-            w1_raw[:].rearrange("p a c -> p (a c)").bitcast(U16).rearrange("p (g m t) -> p g t m", t=PACK, m=P),
-        )
-        nc.vector.tensor_copy(
-            w1_planes[:].rearrange("p (g t m) -> p g t m", t=PACK, m=P),
-            w1_planes_raw[:].rearrange("p a (b m t) -> p (a b) t m", t=PACK, m=P),
-        )
-
         def quantise(grouped, name, width):
             words = keep.tile([P, width], U32, name=f"{name}_words", align_bytes=64)
             plane = keep.tile([P, width], U8, name=f"{name}_plane", align_bytes=64)
             nc.vector.quantize_mx(out=words[:].bitcast(FP8X4), scales=plane[:], in_=grouped[:])
             return words, plane
 
+        by_scalar, by_vector = [nc.scalar.copy], [nc.vector.tensor_copy]
+        by_both = by_scalar + by_vector
+
         def quantise_weight(raw, name, cast):
             grouped = ring.tile([P, PACK * PASS], BF16, name="w_grouped", align_bytes=64, bufs=3)
-            cast(
-                grouped[:].rearrange("p (t m j) -> p m t j", t=PACK, j=PACK),
-                raw[:].rearrange("p j (m t) -> p m t j", t=PACK),
-            )
+            share = P // len(cast)
+            for n, copy in enumerate(cast):
+                copy(
+                    grouped[:].rearrange("p (t m j) -> p m t j", t=PACK, j=PACK)[:, n * share:(n + 1) * share],
+                    raw[:].rearrange("p j (m t) -> p m t j", t=PACK)[:, n * share:(n + 1) * share],
+                )
             return quantise(grouped, name, PASS)
 
         def product(bank, stationary):
@@ -147,12 +161,6 @@ def tile_list_shelf_offer_scores_kernel(
                 )
             return acc
 
-        def w1_tile(b, t):
-            def at(a):
-                c = ((a * NPASS + b) * PACK + t) * P
-                return w1_dealt[:, 2 * c:2 * (c + P)].bitcast(FP4X4), w1_planes[:, c:c + P]
-            return at
-
         def wq_tile(q, b, t):
             def at(a):
                 words, plane = q[a, b]
@@ -162,43 +170,61 @@ def tile_list_shelf_offer_scores_kernel(
         q2, q3, th, turns, whole, cosb, tanh_cos, acc_d, h, picked = ({} for n in range(10))
         TILES = NPASS * PACK
 
+        def tanh_turned(b):
+            th[b] = ring.tile([P, PACK, PACK, P], F32, name="th")
+            for jt in range(S // P):
+                acc = psum.tile([P, PASS], F32, name=f"bank{jt % 2}")
+                for a in range(NPASS):
+                    nc.tensor.matmul_mx(
+                        out=acc[:], lhsT=v_words[a][:, jt * P:(jt + 1) * P].bitcast(FP8X4),
+                        lhsT_scale=v_planes[a][:, jt * P:(jt + 1) * P],
+                        rhs=w1_raw[:, a, 2 * b * PASS:2 * (b + 1) * PASS].bitcast(FP4X4),
+                        rhs_scale=w1_planes_raw[:, a, b * PASS:(b + 1) * PASS],
+                        start=(a == 0), stop=(a == NPASS - 1),
+                    )
+                nc.scalar.activation(th[b][:, jt], acc[:].rearrange("j (p t) -> j t p", t=PACK), ACT.Tanh)
+
         def drain_ab(i):
             b, t = divmod(i, PACK)
             acc_b = product(2 + i % 2, wq_tile(q2, b, t))
-            acc_a = product(4 + i % 2, w1_tile(b, t))
             turns[i] = ring.tile([P, S], F32, name="turns", bufs=4)
             whole[i] = ring.tile([P, S], U32, name="whole", bufs=4)
-            th[i] = ring.tile([P, S], F32, name="th", bufs=4)
             nc.scalar.activation(turns[i][:], acc_b[:], ACT.Abs, scale=1.0 / (2.0 * math.pi))
             nc.scalar.activation(whole[i][:], turns[i][:], ACT.Copy, bias=0.25)
-            nc.scalar.activation(th[i][:], acc_a[:], ACT.Tanh)
 
         def cosine(i):
-            cosb[i] = keep.tile([P, S], F32, name=f"cosb{min(i, PACK - 1)}")
+            cosb[i] = keep.tile([P, S], F32, name=f"cosb{i % PACK}")
             nc.vector.scalar_tensor_tensor(cosb[i][:], turns[i][:], 0.25, whole[i][:].bitcast(I32), ALU.add, ALU.subtract)
             nc.scalar.activation(cosb[i][:], cosb[i][:], ACT.Sin, scale=2.0 * math.pi)
 
         def tanh_times_cos(i):
-            tanh_cos[i] = keep.tile([P, S], F32, name=f"tanh_cos{min(i, PACK - 1)}")
-            nc.vector.tensor_tensor(tanh_cos[i][:], th[i][:], cosb[i][:], ALU.mult)
+            b, t = divmod(i, PACK)
+            turned = psum.tile([P, S], F32, name=f"bank{4 + i % 2}")
+            for jt in range(S // P):
+                nc.tensor.transpose(turned[:, jt * P:(jt + 1) * P], th[b][:, jt, t, :], ident[:])
+            tanh_cos[i] = keep.tile([P, S], F32, name=f"tanh_cos{i % PACK}")
+            nc.vector.tensor_tensor(tanh_cos[i][:], turned[:], cosb[i][:], ALU.mult)
 
         def make_h(i):
             b, t = divmod(i, PACK)
             acc = product(6 + i % 2, wq_tile(q3, b, t))
-            h[i] = keep.tile([P, S], F32, name="h", align_bytes=64)
+            h[i] = keep.tile([P, S], F32, name=f"h{i % 1}", align_bytes=64)
             nc.vector.scalar_tensor_tensor(h[i][:], tanh_cos[i][:], gain_sb[:, b, t:t + 1], acc[:], ALU.mult, ALU.add)
 
         def scatter(i):
             b, t = divmod(i, PACK)
-            nc.vector.tensor_tensor(pages[b, t][:].indirect(list3[:]), h[i][:], wgs_sb[:, t, :], ALU.mult)
+            nc.vector.tensor_tensor(pages[b, t][:].indirect(list3[:]), h[i][:], wgs_sb[t], ALU.mult)
 
         def pick(i):
-            picked[i] = keep.tile([P, S], F32, name="picked", align_bytes=64)
+            picked[i] = keep.tile([P, S], F32, name=f"picked{i % 4}", align_bytes=64)
             nc.vector.tensor_copy(picked[i][:], pages[divmod(i, PACK)][:].indirect(list4[:]))
 
         def floor_at_base(i):
             b, t = divmod(i, PACK)
-            nc.vector.tensor_scalar(x_planes[b][:, t, :], picked[i][:], base_sb[:, b, t:t + 1], None, ALU.max)
+            if t == 0:
+                above[b] = keep.tile([P, PACK, S], F32, name=f"stage{3 - b}")
+            nc.scalar.activation(above[b][:, t, :], picked[i][:], ACT.Relu, bias=neg_base[:, b, t:t + 1])
+            nc.scalar.activation(x_planes[b][:, t, :], above[b][:, t, :], ACT.Identity, bias=base_sb[:, b, t:t + 1])
 
         def interleave_x(b, shares):
             grouped = keep.tile([P, S * PACK], BF16, name="x_grouped", align_bytes=64)
@@ -210,45 +236,45 @@ def tile_list_shelf_offer_scores_kernel(
             return grouped
 
         x_planes = [ring.tile([P, PACK, S], BF16, name="x_planes") for b in range(NPASS)]
-        xq = []
+        xq, above = [], {}
+        neg_base = keep.tile([P, NPASS, PACK], F32, name="neg_base")
+        nc.scalar.activation(neg_base[:], base_sb[:], ACT.Copy, scale=-1.0)
 
-        q2[0, 0] = quantise_weight(raw2[0, 0], "w2_00", nc.scalar.copy)
-        q2[1, 0] = quantise_weight(raw2[1, 0], "w2_10", nc.vector.tensor_copy)
+        q2[0, 0] = quantise_weight(raw2[0, 0], "w2_00", by_scalar)
+        q2[1, 0] = quantise_weight(raw2[1, 0], "w2_10", by_scalar)
+        tanh_turned(0)
         for i in range(PACK):
             drain_ab(i)
             cosine(i)
             tanh_times_cos(i)
             if i == 0:
-                for a in range(NPASS):
-                    q3[a, 0] = quantise_weight(raw3[a, 0], f"w3_{a}0", nc.vector.tensor_copy)
+                q3[0, 0] = quantise_weight(raw3[0, 0], "w3_00", by_vector)
+                q3[1, 0] = quantise_weight(raw3[1, 0], "w3_10", by_vector)
+        v2_plane = keep.tile([P, S2], U8, name="v2_plane", align_bytes=64)
+        nc.vector.tensor_copy(v2_plane[:], tab2_planes[:].indirect(list2[:]))
         for a in range(NPASS):
             raw2[a, 1] = load_weight(w2, a, 1)
         pages[0, 1] = load_page(0, 1)
         for a in range(NPASS):
             raw3[a, 1] = load_weight(w3, a, 1)
-        list2 = load_list("list2", offs2)
-        tab2_w = [load_words("tab_w0", tab2_words[0])]
         pages[0, 2] = load_page(0, 2)
-        for q in range(4):
-            nc.sync.dma_start(
-                tab2_planes[32 * q:32 * q + 8, :].bitcast(I32), tab2_scales[:, 4 * q:4 * q + 4, :].bitcast(I32)
-            )
+        tab2_w = [load_words("tab_w0", tab2_words[0])]
         pages[0, 3] = load_page(0, 3)
         for t in range(PACK):
             pages[1, t] = load_page(1, t)
         tab2_w.append(load_words("tab_w1", tab2_words[1]))
 
         for a in range(NPASS):
-            q2[a, 1] = quantise_weight(raw2[a, 1], f"w2_{a}1", nc.scalar.copy)
+            q2[a, 1] = quantise_weight(raw2[a, 1], f"w2_{a}1", by_scalar)
         for i in range(PACK, TILES):
             drain_ab(i)
             if i == PACK:
                 cosine(i)
+                tanh_turned(1)
                 for a in range(NPASS):
-                    q3[a, 1] = quantise_weight(raw3[a, 1], f"w3_{a}1", nc.scalar.copy)
+                    q3[a, 1] = quantise_weight(raw3[a, 1], f"w3_{a}1", by_scalar)
 
         half = S2 // 2
-        v2_plane = keep.tile([P, S2], U8, name="v2_plane", align_bytes=64)
 
         def gather_v2(name, a, m0, count):
             dst = keep.tile([P, count], U32, name=name, align_bytes=64)
@@ -266,7 +292,7 @@ def tile_list_shelf_offer_scores_kernel(
             if i + 1 < TILES:
                 make_h(i + 1)
             else:
-                gather_v2("h", 0, half, half)
+                gather_v2(f"h{(TILES - 1) % 1}", 0, half, half)
             pick(i)
             if PACK <= i + 2 < TILES:
                 tanh_times_cos(i + 2)
@@ -276,13 +302,12 @@ def tile_list_shelf_offer_scores_kernel(
             if i == PACK - 1:
                 xq.append(quantise(interleave_x(0, [(nc.scalar.copy, 0, S)]), "x0", S))
             if i == PACK:
-                nc.vector.tensor_copy(v2_plane[:], tab2_planes[:].indirect(list2[:]))
                 gather_v2("v2_early", 0, 0, half)
 
+        gather_v2("page13", 1, 0, half)
         grouped = interleave_x(1, [(nc.scalar.copy, 0, S // 2), (nc.vector.tensor_copy, S // 2, S)])
-        gather_v2("picked", 1, 0, SLICE)
         xq.append(quantise(grouped, "x1", S))
-        gather_v2("x_grouped", 1, SLICE, S2 - SLICE)
+        gather_v2("x_grouped", 1, half, half)
 
         acc_e = [psum.tile([P, S], F32, name=f"bank{m}") for m in range(S2 // P)]
 
@@ -300,6 +325,6 @@ def tile_list_shelf_offer_scores_kernel(
             score_pass(m, 1, vq[1])
             score_pass(m, 1, xq[1], stop=True)
             if m % 2 == 0:
-                res = ring.tile([P, 2, S], F32, name="w_raw", bufs=4)
+                res = keep.tile([P, 2, S], F32, name=f"stage{m // 2}")
             nc.scalar.activation(res[:, m % 2, :], acc_e[m][:], ACT.Tanh)
             nc.sync.dma_start(out[m * P:(m + 1) * P, :], res[:, m % 2, :])

import math
from contextlib import ExitStack

import concourse.mybir as mybir
from concourse.masks import make_identity

F32 = mybir.dt.float32
BF16 = mybir.dt.bfloat16
I32 = mybir.dt.int32
U32 = mybir.dt.uint32
U16 = mybir.dt.uint16
U8 = mybir.dt.uint8
FP8X4 = mybir.dt.float8_e4m3fn_x4
FP4X4 = mybir.dt.float4_e2m1fn_x4
ACT = mybir.ActivationFunctionType
ALU = mybir.AluOpType

P = 128
PACK = 4
PASS = P * PACK
K = 1024
T = 2048
S = 512
S2 = 1024
T2 = 1024
NPASS = K // PASS
SLICE = 256

FLOPS = 5368709120


def tile_list_shelf_offer_scores_kernel(
    tc, tab_words, tab_scales, offs, tab2_words, tab2_scales, offs2, w1_words, w1_scales,
    w2, w3, gain, page0, wgs, offs3, offs4, base, out,
):
    nc = tc.nc
    with ExitStack() as ctx:
        keep = ctx.enter_context(tc.tile_pool(name="keep", bufs=1))
        ring = ctx.enter_context(tc.tile_pool(name="ring", bufs=2))
        psum = ctx.enter_context(tc.psum_pool(name="psum", bufs=1))

        def load_list(name, src):
            t = keep.tile(list(src.shape), U16, name=name)
            nc.sync.dma_start(t[:], src)
            return t

        def load_words(name, src):
            t = keep.tile([P, T], I32, name=name)
            nc.sync.dma_start(t[:], src.rearrange("p t i -> p (t i)").bitcast(I32))
            return t

        def zeroed_planes(name, shape):
            t = keep.tile(shape, U8, name=name, align_bytes=64)
            nc.vector.memset(t[:].bitcast(I32), 0)
            return t

        def load_planes(t, src):
            for r in range(4):
                nc.sync.dma_start(
                    t[r:P:32].bitcast(I32), src[:, r:16:4, :].rearrange("a q c -> q a c").bitcast(I32)
                )

        staged = []

        def load_weight(w, a, b):
            raw = keep.tile([P, PACK, PASS], F32, name=f"stage{len(staged) % 4}")
            staged.append(raw)
            nc.sync.dma_start(
                raw[:], w[a * PASS:(a + 1) * PASS, b * PASS:(b + 1) * PASS].rearrange("(p j) c -> p j c", j=PACK)
            )
            return raw

        def load_page(b, t):
            page = keep.tile([P, T2], F32, name=f"page{b}{t}", align_bytes=64)
            nc.sync.dma_start(page[:], page0[b * PASS + t:(b + 1) * PASS:PACK, :])
            return page

        tab_planes = keep.tile([P, NPASS, T], U8, name="tab_planes", align_bytes=64)
        nc.vector.memset(tab_planes[:, 0, :].bitcast(I32), 0)
        nc.gpsimd.memset(tab_planes[:, 1, :].bitcast(I32), 0)
        warm = keep.tile([P, 2], F32, name="warm")
        nc.gpsimd.memset(warm[:, 0:1], 0.0)
        nc.scalar.activation(warm[:, 1:2], warm[:, 0:1], ACT.Silu)

        tab2_planes = zeroed_planes("tab2_planes", [P, T])
        w1_planes_raw = zeroed_planes("w1_planes_raw", [P, NPASS, K])

        ident = keep.tile([P, P], F32, name="ident")
        make_identity(nc, ident[:])

        gain_sb = keep.tile([P, NPASS, PACK], F32, name="gain_sb")
        base_sb = keep.tile([P, NPASS, PACK], F32, name="base_sb")

        raw2 = {}
        tab_w = [load_words("tab_w0", tab_words[0])]
        list1 = load_list("list1", offs)
        load_planes(tab_planes, tab_scales)
        raw2[0, 0] = load_weight(w2, 0, 0)
        list2 = load_list("list2", offs2)
        for q in range(4):
            nc.sync.dma_start(
                tab2_planes[32 * q:32 * q + 8, :].bitcast(I32), tab2_scales[:, 4 * q:4 * q + 4, :].bitcast(I32)
            )
        raw2[1, 0] = load_weight(w2, 1, 0)
        tab_w.append(load_words("tab_w1", tab_words[1]))
        w1_raw = keep.tile([P, NPASS, 2 * K], U8, name="w1_raw", align_bytes=64)
        nc.sync.dma_start(w1_raw[:].bitcast(I32), w1_words.rearrange("a p c -> p a c").bitcast(I32))
        load_planes(w1_planes_raw, w1_scales)
        raw3 = {(0, 0): load_weight(w3, 0, 0)}
        nc.sync.dma_start(gain_sb[:], gain.rearrange("(b p t) -> p b t", p=P, t=PACK))
        raw3[1, 0] = load_weight(w3, 1, 0)
        list3 = load_list("list3", offs3)
        wgs_rows = wgs.rearrange("(p t) j -> p t j", t=PACK)
        wgs_first = keep.tile([P, 1, S], F32, name="wgs_first")
        wgs_rest = keep.tile([P, PACK - 1, S], F32, name="wgs_rest")
        wgs_sb = [wgs_first[:, 0, :]] + [wgs_rest[:, t, :] for t in range(PACK - 1)]
        for q in (0, 2, 1, 3):
            nc.sync.dma_start(wgs_first[32 * q:32 * q + 32], wgs_rows[:, 0:1, :])
        pages = {(0, 0): load_page(0, 0)}
        for q in (0, 2, 1, 3):
            nc.sync.dma_start(wgs_rest[32 * q:32 * q + 32], wgs_rows[:, 1:PACK, :])
        list4 = load_list("list4", offs4)
        nc.sync.dma_start(base_sb[:], base.rearrange("(b p t) -> p b t", p=P, t=PACK))

        v_words, v_planes = [], []
        for a in range(NPASS):
            words = keep.tile([P, S], U32, name=f"v_words{a}", align_bytes=64)
            plane = keep.tile([P, S], U8, name=f"v_plane{a}", align_bytes=64)
            nc.vector.tensor_copy(words[:], tab_w[a][:].bitcast(U32).indirect(list1[:]))
            nc.vector.tensor_copy(plane[:], tab_planes[:, a, :].indirect(list1[:]))
            v_words.append(words)
            v_planes.append(plane)

        def quantise(grouped, name, width):
            words = keep.tile([P, width], U32, name=f"{name}_words", align_bytes=64)
            plane = keep.tile([P, width], U8, name=f"{name}_plane", align_bytes=64)
            nc.vector.quantize_mx(out=words[:].bitcast(FP8X4), scales=plane[:], in_=grouped[:])
            return words, plane

        by_scalar, by_vector = [nc.scalar.copy], [nc.vector.tensor_copy]
        by_both = by_scalar + by_vector

        def quantise_weight(raw, name, cast):
            grouped = ring.tile([P, PACK * PASS], BF16, name="w_grouped", align_bytes=64, bufs=3)
            share = P // len(cast)
            for n, copy in enumerate(cast):
                copy(
                    grouped[:].rearrange("p (t m j) -> p m t j", t=PACK, j=PACK)[:, n * share:(n + 1) * share],
                    raw[:].rearrange("p j (m t) -> p m t j", t=PACK)[:, n * share:(n + 1) * share],
                )
            return quantise(grouped, name, PASS)

        def product(bank, stationary):
            acc = psum.tile([P, S], F32, name=f"bank{bank}")
            for a in range(NPASS):
                words, plane = stationary(a)
                nc.tensor.matmul_mx(
                    out=acc[:], lhsT=words, lhsT_scale=plane,
                    rhs=v_words[a][:].bitcast(FP8X4), rhs_scale=v_planes[a][:],
                    start=(a == 0), stop=(a == NPASS - 1),
                )
            return acc

        def wq_tile(q, b, t):
            def at(a):
                words, plane = q[a, b]
                return words[:, t * P:(t + 1) * P].bitcast(FP8X4), plane[:, t * P:(t + 1) * P]
            return at

        q2, q3, th, turns, whole, cosb, tanh_cos, acc_d, h, picked = ({} for n in range(10))
        TILES = NPASS * PACK

        def tanh_turned(b):
            th[b] = ring.tile([P, PACK, PACK, P], F32, name="th")
            for jt in range(S // P):
                acc = psum.tile([P, PASS], F32, name=f"bank{jt % 2}")
                for a in range(NPASS):
                    nc.tensor.matmul_mx(
                        out=acc[:], lhsT=v_words[a][:, jt * P:(jt + 1) * P].bitcast(FP8X4),
                        lhsT_scale=v_planes[a][:, jt * P:(jt + 1) * P],
                        rhs=w1_raw[:, a, 2 * b * PASS:2 * (b + 1) * PASS].bitcast(FP4X4),
                        rhs_scale=w1_planes_raw[:, a, b * PASS:(b + 1) * PASS],
                        start=(a == 0), stop=(a == NPASS - 1),
                    )
                nc.scalar.activation(th[b][:, jt], acc[:].rearrange("j (p t) -> j t p", t=PACK), ACT.Tanh)

        def drain_ab(i):
            b, t = divmod(i, PACK)
            acc_b = product(2 + i % 2, wq_tile(q2, b, t))
            turns[i] = ring.tile([P, S], F32, name="turns", bufs=4)
            whole[i] = ring.tile([P, S], U32, name="whole", bufs=4)
            nc.scalar.activation(turns[i][:], acc_b[:], ACT.Abs, scale=1.0 / (2.0 * math.pi))
            nc.scalar.activation(whole[i][:], turns[i][:], ACT.Copy, bias=0.25)

        def cosine(i):
            cosb[i] = keep.tile([P, S], F32, name=f"cosb{i % PACK}")
            nc.vector.scalar_tensor_tensor(cosb[i][:], turns[i][:], 0.25, whole[i][:].bitcast(I32), ALU.add, ALU.subtract)
            nc.scalar.activation(cosb[i][:], cosb[i][:], ACT.Sin, scale=2.0 * math.pi)

        def tanh_times_cos(i):
            b, t = divmod(i, PACK)
            turned = psum.tile([P, S], F32, name=f"bank{4 + i % 2}")
            for jt in range(S // P):
                nc.tensor.transpose(turned[:, jt * P:(jt + 1) * P], th[b][:, jt, t, :], ident[:])
            tanh_cos[i] = keep.tile([P, S], F32, name=f"tanh_cos{i % PACK}")
            nc.vector.tensor_tensor(tanh_cos[i][:], turned[:], cosb[i][:], ALU.mult)

        def make_h(i):
            b, t = divmod(i, PACK)
            acc = product(6 + i % 2, wq_tile(q3, b, t))
            h[i] = keep.tile([P, S], F32, name=f"h{i % 1}", align_bytes=64)
            nc.vector.scalar_tensor_tensor(h[i][:], tanh_cos[i][:], gain_sb[:, b, t:t + 1], acc[:], ALU.mult, ALU.add)

        def scatter(i):
            b, t = divmod(i, PACK)
            nc.vector.tensor_tensor(pages[b, t][:].indirect(list3[:]), h[i][:], wgs_sb[t], ALU.mult)

        def pick(i):
            picked[i] = keep.tile([P, S], F32, name=f"picked{i % 4}", align_bytes=64)
            nc.vector.tensor_copy(picked[i][:], pages[divmod(i, PACK)][:].indirect(list4[:]))

        def floor_at_base(i):
            b, t = divmod(i, PACK)
            if t == 0:
                above[b] = keep.tile([P, PACK, S], F32, name=f"stage{3 - b}")
            nc.scalar.activation(above[b][:, t, :], picked[i][:], ACT.Relu, bias=neg_base[:, b, t:t + 1])
            nc.scalar.activation(x_planes[b][:, t, :], above[b][:, t, :], ACT.Identity, bias=base_sb[:, b, t:t + 1])

        def interleave_x(b, shares):
            grouped = keep.tile([P, S * PACK], BF16, name="x_grouped", align_bytes=64)
            for copy, j0, j1 in shares:
                copy(
                    grouped[:, j0 * PACK:j1 * PACK].rearrange("p (c i t) -> p c t i", i=4, t=PACK),
                    x_planes[b][:, :, j0:j1].rearrange("p t (c i) -> p c t i", i=4),
                )
            return grouped

        x_planes = [ring.tile([P, PACK, S], BF16, name="x_planes") for b in range(NPASS)]
        xq, above = [], {}
        neg_base = keep.tile([P, NPASS, PACK], F32, name="neg_base")
        nc.scalar.activation(neg_base[:], base_sb[:], ACT.Copy, scale=-1.0)

        q2[0, 0] = quantise_weight(raw2[0, 0], "w2_00", by_scalar)
        q2[1, 0] = quantise_weight(raw2[1, 0], "w2_10", by_scalar)
        tanh_turned(0)
        for i in range(PACK):
            drain_ab(i)
            cosine(i)
            tanh_times_cos(i)
            if i == 0:
                q3[0, 0] = quantise_weight(raw3[0, 0], "w3_00", by_vector)
                q3[1, 0] = quantise_weight(raw3[1, 0], "w3_10", by_vector)
        v2_plane = keep.tile([P, S2], U8, name="v2_plane", align_bytes=64)
        nc.vector.tensor_copy(v2_plane[:], tab2_planes[:].indirect(list2[:]))
        for a in range(NPASS):
            raw2[a, 1] = load_weight(w2, a, 1)
        pages[0, 1] = load_page(0, 1)
        for a in range(NPASS):
            raw3[a, 1] = load_weight(w3, a, 1)
        pages[0, 2] = load_page(0, 2)
        tab2_w = [load_words("tab_w0", tab2_words[0])]
        pages[0, 3] = load_page(0, 3)
        for t in range(PACK):
            pages[1, t] = load_page(1, t)
        tab2_w.append(load_words("tab_w1", tab2_words[1]))

        for a in range(NPASS):
            q2[a, 1] = quantise_weight(raw2[a, 1], f"w2_{a}1", by_scalar)
        for i in range(PACK, TILES):
            drain_ab(i)
            if i == PACK:
                cosine(i)
                tanh_turned(1)
                for a in range(NPASS):
                    q3[a, 1] = quantise_weight(raw3[a, 1], f"w3_{a}1", by_scalar)

        half = S2 // 2

        def gather_v2(name, a, m0, count):
            dst = keep.tile([P, count], U32, name=name, align_bytes=64)
            for c in range(0, count, SLICE if a else half):
                n = SLICE if a else half
                part = list2[:, (m0 + c) // 16:(m0 + c + n) // 16]
                nc.vector.tensor_copy(dst[:, c:c + n], tab2_w[a][:].bitcast(U32).indirect(part))
            for c in range(0, count, P):
                v2_words[a, (m0 + c) // P] = dst[:, c:c + P]

        v2_words = {}
        make_h(0)
        for i in range(TILES):
            scatter(i)
            if i + 1 < TILES:
                make_h(i + 1)
            else:
                gather_v2(f"h{(TILES - 1) % 1}", 0, half, half)
            pick(i)
            if PACK <= i + 2 < TILES:
                tanh_times_cos(i + 2)
            floor_at_base(i)
            if PACK < i + 3 < TILES:
                cosine(i + 3)
            if i == PACK - 1:
                xq.append(quantise(interleave_x(0, [(nc.scalar.copy, 0, S)]), "x0", S))
            if i == PACK:
                gather_v2("v2_early", 0, 0, half)

        gather_v2("page13", 1, 0, half)
        grouped = interleave_x(1, [(nc.scalar.copy, 0, S // 2), (nc.vector.tensor_copy, S // 2, S)])
        xq.append(quantise(grouped, "x1", S))
        gather_v2("x_grouped", 1, half, half)

        acc_e = [psum.tile([P, S], F32, name=f"bank{m}") for m in range(S2 // P)]

        def score_pass(m, a, moving, start=False, stop=False):
            nc.tensor.matmul_mx(
                out=acc_e[m][:], lhsT=v2_words[a, m].bitcast(FP8X4), lhsT_scale=v2_plane[4 * a:P, m * P:(m + 1) * P],
                rhs=moving[0][:].bitcast(FP8X4), rhs_scale=moving[1][:], start=start, stop=stop,
            )

        vq = list(zip(v_words, v_planes))
        for m in range(8):
            score_pass(m, 0, vq[0], start=True)
            score_pass(m, 0, xq[0])
        for m in range(8):
            score_pass(m, 1, vq[1])
            score_pass(m, 1, xq[1], stop=True)
            if m % 2 == 0:
                res = keep.tile([P, 2, S], F32, name=f"stage{m // 2}")
            nc.scalar.activation(res[:, m % 2, :], acc_e[m][:], ACT.Tanh)
            nc.sync.dma_start(out[m * P:(m + 1) * P, :], res[:, m % 2, :])
